import numpy as np, ml_dtypes
CORES = [56,64,184,192,312,320,440,448]
N = 8
S, B = 2, 128
def setup_inputs(rng):
    a = (rng.standard_normal((128, 128), dtype=np.float32) / 12).astype(ml_dtypes.bfloat16)
    return {"x": rng.standard_normal((N, 128, S * B), dtype=np.float32).astype(ml_dtypes.bfloat16), "a": np.broadcast_to(a, (N, 128, 128)).copy(), "at": np.broadcast_to(a.T, (N, 128, 128)).copy()}
def setup_inputs_big(rng):
    d = setup_inputs(rng)
    for k in ("x",): d[k] = (d[k].astype(np.float32) * 1048576.0).astype(d[k].dtype)
    return d
def setup_inputs_small(rng):
    d = setup_inputs(rng)
    for k in ("x",): d[k] = (d[k].astype(np.float32) * (1 / 1048576.0)).astype(d[k].dtype)
    return d
def setup_inputs_apart(rng):
    d = setup_inputs(rng)
    f = (10.0 ** rng.permutation(np.linspace(-1.5, 1.5, N))).astype(np.float32).reshape(N, 1, 1)
    for k in ("x",): d[k] = (d[k].astype(np.float32) * f).astype(d[k].dtype)
    return d
def reference(x, a, at):
    X, A = x.astype(np.float64), a.astype(np.float64)
    y = np.zeros((N, 128, S * B)); h = np.zeros((128, B))
    for r in range(N):
        for s in range(S):
            h = A[r].T @ h + X[r][:, B * s:B * s + B]
            y[r][:, B * s:B * s + B] = h
    return {"y": y.astype(ml_dtypes.bfloat16)}

@@ -1,0 +1,251 @@
+from concourse.bass import DstId, RemoteDMATransfer
+from concourse.mybir import AluOpType
+
+N, S, B = 8, 2, 128
+WORLD = 512
+NPOW = S * (N - 1)
+FAN = 2
+NE_OFF = 8
+NE_ON = 8
+STEP = 1
+OTHER_DIE = ()
+LEVELS = 4
+
+SCRATCH = {
+    "xs": ("sbuf", [128, S * B], "bfloat16"),
+    "pw": ("sbuf", [128, NPOW * B], "bfloat16"),
+    "tp": ("sbuf", [128, LEVELS * B], "bfloat16"),
+    "land": ("sbuf", [128, (N - 1) * B], "bfloat16"),
+    "ys": ("sbuf", [128, S * B], "bfloat16"),
+    "pc": ("psum", [128, 512], "float32"),
+    "py0": ("psum", [128, 512], "float32"),
+    "py1": ("psum", [128, 512], "float32"),
+    "pa0": ("psum", [128, 512], "float32"),
+    "pa1": ("psum", [128, 512], "float32"),
+    "pt0": ("psum", [128, 512], "float32"),
+    "pt1": ("psum", [128, 512], "float32"),
+}
+SEMAPHORES = (["ldx", "lda", "ldt", "mmc", "car", "my0", "my1", "vy0", "vy1", "st0", "st1", "loc"]
+              + ["arr%d" % s for s in range(N - 1)]
+              + ["%s%d" % (n, l) for l in range(LEVELS) for n in ("ma", "mt", "ca", "ct")])
+
+_CACHE = {}
+
+
+def _same_chip(topo, a, b):
+    return topo.host(a) == topo.host(b) and topo.chip(a) == topo.chip(b)
+
+
+def _engines(topo, src, dsts, count, avoid):
+    m = topo.mask(src, dsts[0])
+    for d in dsts[1:]:
+        m &= topo.mask(src, d)
+    free = [i for i in range(m.bit_length()) if (m >> i) & 1 and not (avoid >> i) & 1]
+    out = 0
+    for i in free[::STEP][:count]:
+        out |= 1 << i
+    return out
+
+
+def _plan(cores, topo):
+    n = len(cores)
+    ok = topo.may_write
+    chipc = [[k for k in range(WORLD) if k != c and _same_chip(topo, k, c)] for c in cores]
+    used = []
+
+    def pick(m, srcs, dsts):
+        cand = [k for k in chipc[m] if k not in used and all(ok(s, k) for s in srcs) and all(ok(k, d) for d in dsts)]
+        cand.sort(key=lambda k: ((topo.die(k) != topo.die(cores[m])) != (m in OTHER_DIE), k))
+        used.append(cand[0])
+        return cand[0]
+
+    far, via = {}, {}
+    for j in range(n - 1):
+        f = [r for r in range(j + 1, n)
+             if not ok(cores[j], cores[r]) and not any(ok(k, cores[r]) for k in chipc[j])]
+        if f:
+            far[j] = f
+            via[j] = min(m for m in range(j + 1, f[0])
+                         if any(ok(cores[j], k) and all(ok(k, cores[r]) for r in f) for k in chipc[m]))
+    order = []
+    for j in range(n - 1):
+        k = j
+        while k is not None and k not in order:
+            order.append(k)
+            k = via.get(k)
+    slot = {j: s for s, j in enumerate(order)}
+
+    first = {j: [[], []] for j in range(n)}
+    late = {j: [] for j in range(n)}
+    hcalls = {}
+    fwd = {}
+    covered = []
+    for j in sorted(via):
+        m = via[j]
+        own = [r for r in far[j] if ok(cores[m], cores[r])]
+        oth = [r for r in far[j] if r not in own]
+        if oth:
+            h = pick(m, [cores[j], cores[m]], [cores[r] for r in oth])
+            hcalls[h] = (30, [slot[j], slot[m]], slot[j], 2, oth)
+            first[j][1].append(h)
+            late[m].append(h)
+            covered += [(j, r) for r in oth] + [(m, r) for r in oth]
+        if own:
+            fwd[m] = (slot[j], own)
+            first[j][1].append(cores[m])
+            covered += [(j, r) for r in own] + [(j, m)]
+    direct = {}
+    for j in range(n - 1):
+        rest = [r for r in range(j + 1, n) if (j, r) not in covered]
+        direct[j] = [r for r in rest if ok(cores[j], cores[r])]
+        near = [r for r in rest if r not in direct[j]]
+        for i in range(0, len(near), FAN):
+            dst = near[i:i + FAN]
+            h = pick(j, [cores[j]], [cores[r] for r in dst])
+            hcalls[h] = (20, [slot[j]], slot[j], 1, dst)
+            first[j][0].append(h)
+        first[j][0] += late[j]
+
+    calls, lands = {}, {}
+
+    def add(core, needs, trs, score):
+        calls.setdefault(core, []).append((needs, trs))
+        for s0, ns, dsts, mask in trs:
+            for p, d in enumerate(dsts):
+                lands.setdefault(d, []).append((score + p, s0, ns, bin(mask).count("1")))
+
+    for j in range(n - 1):
+        c, trs, off = cores[j], [], 0
+        if first[j][1]:
+            off = _engines(topo, c, first[j][1], NE_OFF, 0)
+            trs.append((slot[j], 1, first[j][1], off))
+        if first[j][0]:
+            trs.append((slot[j], 1, first[j][0], _engines(topo, c, first[j][0], NE_ON, off)))
+        if trs:
+            add(c, [], trs, 0)
+        if direct[j]:
+            dst = [cores[r] for r in direct[j]]
+            add(c, [], [(slot[j], 1, dst, _engines(topo, c, dst, NE_OFF, 0))], 5)
+        if j in fwd:
+            dst = [cores[r] for r in fwd[j][1]]
+            add(c, [fwd[j][0]], [(fwd[j][0], 1, dst, _engines(topo, c, dst, NE_OFF, 0))], 10)
+    for h, (score, needs, s0, ns, dst) in hcalls.items():
+        dst = [cores[r] for r in dst]
+        add(h, needs, [(s0, ns, dst, _engines(topo, h, dst, NE_OFF, 0))], score)
+    return slot, calls, lands
+
+
+def _send(g, core, T, topo, calls, lands):
+    count = {s0: k for _, s0, _, k in lands}
+    total = 0
+    for needs, trs in calls:
+        for s in needs:
+            g.wait_ge(T.sem["arr%d" % s], count[s])
+        lst = []
+        for s0, ns, dsts, mask in trs:
+            ap = T.land[:, s0 * B:(s0 + ns) * B]
+            ids = []
+            for d in dsts:
+                rid, pid = topo.addr(d, core)
+                ids.append(DstId(rid=rid, pnc=pid))
+            lst.append(RemoteDMATransfer(dst_ids=ids, dma_engine_mask=mask, remote_sem=T.sem["arr%d" % s0],
+                                         srcs=[ap], dsts=[ap for _ in dsts], alu_op=0))
+            total += bin(mask).count("1")
+        g.remote_dma_fused(lst, local_sem=T.sem.loc)
+    if total:
+        g.wait_ge(T.sem.loc, total)
+
+
+def rank_program(g, core, T, topo):
+    if "p" not in _CACHE:
+        _CACHE["p"] = _plan(list(T.cores), topo)
+    slot, calls, lands = _CACHE["p"]
+    rank = T.rank_of(core)
+    if rank is None:
+        if core in calls:
+            _send(g, core, T, topo, calls[core], lands[core])
+        return
+
+    sem, te, ve, sy, sc = T.sem, g.tensor, g.vector, g.sync, g.scalar
+    x0, x1 = T.xs[:, 0:B], T.xs[:, B:2 * B]
+    top = S * rank
+
+    def pw(lo, hi):
+        return T.pw[:, (lo - 1) * B:hi * B]
+
+    def tp(i):
+        return T.tp[:, i * B:(i + 1) * B]
+
+    sy.dma_start(T.xs[:], T.x[:]).then_inc(sem.ldx, 16)
+    sc.dma_start(pw(1, 1), T.a[:]).then_inc(sem.lda, 16)
+    if top:
+        sc.dma_start(tp(0), T.at[:]).then_inc(sem.ldt, 16)
+
+    te.wait_ge(sem.ldx, 16)
+    te.wait_ge(sem.lda, 16)
+    ve.wait_ge(sem.ldx, 16)
+    if rank < N - 1:
+        mine = T.land[:, slot[rank] * B:(slot[rank] + 1) * B]
+        te.matmul(T.pc[:, 0:B], pw(1, 1), x0, True, True).then_inc(sem.mmc, 1)
+        ve.wait_ge(sem.mmc, 1)
+        ve.tensor_tensor(mine, T.pc[:, 0:B], x1, AluOpType.add).then_inc(sem.car, 1)
+        g.wait_ge(sem.car, 1)
+        _send(g, core, T, topo, calls[core], lands.get(core, []))
+
+    if rank == 0:
+        sy.wait_ge(sem.ldx, 16)
+        sy.dma_start(T.y[:, 0:B], x0).then_inc(sem.st0, 16)
+        sy.wait_ge(sem.st0, 16)
+        sc.wait_ge(sem.car, 1)
+        sc.dma_start(T.y[:, B:2 * B], mine).then_inc(sem.st1, 16)
+        sc.wait_ge(sem.st1, 16)
+        return
+
+    done = [0, 1]
+    te.matmul(T.py1[:, 0:B], pw(1, 1), x0, True, False).then_inc(sem.my1, 1)
+
+    te.wait_ge(sem.ldt, 16)
+    have, l = 1, 0
+    while have < top:
+        hi = min(2 * have, top)
+        mid = min(hi, have + 4)
+        pa, pt = T["pa%d" % (l % 2)], T["pt%d" % (l % 2)]
+        te.matmul(pa[:, 0:(mid - have) * B], tp(l), pw(1, mid - have), True, True).then_inc(sem["ma%d" % l], 1)
+        ve.wait_ge(sem["ma%d" % l], 1)
+        ve.tensor_copy(pw(have + 1, mid), pa[:, 0:(mid - have) * B]).then_inc(sem["ca%d" % l], 1)
+        second = None
+        if hi > mid:
+            second = (pw(mid + 1, hi), pt[:, 0:(hi - mid) * B])
+            te.matmul(second[1], tp(l), pw(mid - have + 1, hi - have), True, True).then_inc(sem["mt%d" % l], 1)
+        elif hi < top:
+            second = (tp(l + 1), pt[:, 0:B])
+            te.matmul(second[1], pw(have, have), tp(l), True, True).then_inc(sem["mt%d" % l], 1)
+        if second:
+            ve.wait_ge(sem["mt%d" % l], 1)
+            ve.tensor_copy(second[0], second[1]).then_inc(sem["ct%d" % l], 1)
+            te.wait_ge(sem["ct%d" % l], 1)
+        te.wait_ge(sem["ca%d" % l], 1)
+        have, l = hi, l + 1
+
+    piece = {s: j for j, s in slot.items()}
+    seq = sorted(lands[core])
+    for i, (_, s0, ns, cnt) in enumerate(seq):
+        te.wait_ge(sem["arr%d" % s0], cnt)
+        for half in range(S):
+            for s in range(s0, s0 + ns):
+                k = S * (rank - 1 - piece[s]) + 1 + half
+                last = i == len(seq) - 1 and s == s0 + ns - 1
+                te.matmul(T["py%d" % half][:, 0:B], pw(k, k), T.land[:, s * B:(s + 1) * B],
+                          done[half] == 0, last).then_inc(sem["my%d" % half], 1)
+                done[half] += 1
+
+    ve.wait_ge(sem.my0, done[0])
+    ve.tensor_tensor(T.ys[:, 0:B], T.py0[:, 0:B], x0, AluOpType.add).then_inc(sem.vy0, 1)
+    ve.wait_ge(sem.my1, done[1])
+    ve.tensor_tensor(T.ys[:, B:2 * B], T.py1[:, 0:B], x1, AluOpType.add).then_inc(sem.vy1, 1)
+    sy.wait_ge(sem.vy0, 1)
+    sy.dma_start(T.y[:, 0:B], T.ys[:, 0:B]).then_inc(sem.st0, 16)
+    sy.wait_ge(sem.st0, 16)
+    sc.wait_ge(sem.vy1, 1)
+    sc.dma_start(T.y[:, B:2 * B], T.ys[:, B:2 * B]).then_inc(sem.st1, 16)
+    sc.wait_ge(sem.st1, 16)

@@ -7,17 +7,18 @@ NPOW = S * (N - 1)
 FAN = 2
 NE_OFF = 8
 NE_ON = 8
-STEP = 1
-OTHER_DIE = ()
 LEVELS = 4
+NSLOT = 3 * (N - 1)
 
 SCRATCH = {
     "xs": ("sbuf", [128, S * B], "bfloat16"),
     "pw": ("sbuf", [128, NPOW * B], "bfloat16"),
     "tp": ("sbuf", [128, LEVELS * B], "bfloat16"),
-    "land": ("sbuf", [128, (N - 1) * B], "bfloat16"),
+    "land": ("sbuf", [128, NSLOT * B], "bfloat16"),
+    "es": ("sbuf", [128, B], "bfloat16"),
     "ys": ("sbuf", [128, S * B], "bfloat16"),
     "pc": ("psum", [128, 512], "float32"),
+    "pd": ("psum", [128, 512], "float32"),
     "py0": ("psum", [128, 512], "float32"),
     "py1": ("psum", [128, 512], "float32"),
     "pa0": ("psum", [128, 512], "float32"),
@@ -25,8 +26,8 @@ SCRATCH = {
     "pt0": ("psum", [128, 512], "float32"),
     "pt1": ("psum", [128, 512], "float32"),
 }
-SEMAPHORES = (["ldx", "lda", "ldt", "mmc", "car", "my0", "my1", "vy0", "vy1", "st0", "st1", "loc"]
-              + ["arr%d" % s for s in range(N - 1)]
+SEMAPHORES = (["ldx", "lda", "ldt", "mmc", "car", "mq", "cq", "md", "dd", "my0", "my1", "vy0", "vy1", "st0", "st1", "loc"]
+              + ["arr%d" % s for s in range(NSLOT)]
               + ["%s%d" % (n, l) for l in range(LEVELS) for n in ("ma", "mt", "ca", "ct")])
 
 _CACHE = {}
@@ -42,7 +43,7 @@ def _engines(topo, src, dsts, count, avoid):
         m &= topo.mask(src, d)
     free = [i for i in range(m.bit_length()) if (m >> i) & 1 and not (avoid >> i) & 1]
     out = 0
-    for i in free[::STEP][:count]:
+    for i in free[:count]:
         out |= 1 << i
     return out
 
@@ -53,103 +54,151 @@ def _plan(cores, topo):
     chipc = [[k for k in range(WORLD) if k != c and _same_chip(topo, k, c)] for c in cores]
     used = []
 
+    def cs(j):
+        return j
+
+    def ds(j):
+        return n - 1 + j
+
+    def fs(j):
+        return 2 * (n - 1) + j
+
     def pick(m, srcs, dsts):
         cand = [k for k in chipc[m] if k not in used and all(ok(s, k) for s in srcs) and all(ok(k, d) for d in dsts)]
-        cand.sort(key=lambda k: ((topo.die(k) != topo.die(cores[m])) != (m in OTHER_DIE), k))
+        cand.sort(key=lambda k: (topo.die(k) != topo.die(cores[m]), k))
         used.append(cand[0])
         return cand[0]
 
-    far, via = {}, {}
-    for j in range(n - 1):
-        f = [r for r in range(j + 1, n)
-             if not ok(cores[j], cores[r]) and not any(ok(k, cores[r]) for k in chipc[j])]
-        if f:
-            far[j] = f
-            via[j] = min(m for m in range(j + 1, f[0])
-                         if any(ok(cores[j], k) and all(ok(k, cores[r]) for r in f) for k in chipc[m]))
-    order = []
-    for j in range(n - 1):
-        k = j
-        while k is not None and k not in order:
-            order.append(k)
-            k = via.get(k)
-    slot = {j: s for s, j in enumerate(order)}
+    cls = list(range(n))
+    for i in range(n):
+        for j in range(i):
+            if ok(cores[j], cores[i]) and cls[i] != cls[j]:
+                old, new = cls[i], cls[j]
+                cls = [new if c == old else c for c in cls]
 
-    first = {j: [[], []] for j in range(n)}
-    late = {j: [] for j in range(n)}
-    hcalls = {}
+    direct = {j: [] for j in range(n)}
     fwd = {}
-    covered = []
-    for j in sorted(via):
-        m = via[j]
-        own = [r for r in far[j] if ok(cores[m], cores[r])]
-        oth = [r for r in far[j] if r not in own]
-        if oth:
-            h = pick(m, [cores[j], cores[m]], [cores[r] for r in oth])
-            hcalls[h] = (30, [slot[j], slot[m]], slot[j], 2, oth)
-            first[j][1].append(h)
-            late[m].append(h)
-            covered += [(j, r) for r in oth] + [(m, r) for r in oth]
-        if own:
-            fwd[m] = (slot[j], own)
-            first[j][1].append(cores[m])
-            covered += [(j, r) for r in own] + [(j, m)]
-    direct = {}
-    for j in range(n - 1):
-        rest = [r for r in range(j + 1, n) if (j, r) not in covered]
-        direct[j] = [r for r in rest if ok(cores[j], cores[r])]
-        near = [r for r in rest if r not in direct[j]]
-        for i in range(0, len(near), FAN):
-            dst = near[i:i + FAN]
-            h = pick(j, [cores[j]], [cores[r] for r in dst])
-            hcalls[h] = (20, [slot[j]], slot[j], 1, dst)
-            first[j][0].append(h)
-        first[j][0] += late[j]
+    want = {}
+    single = {j: [] for j in range(n)}
+    for r in range(n):
+        own = [j for j in range(r) if cls[j] == cls[r]]
+        oth = [j for j in range(r) if cls[j] != cls[r]]
+        for j in own:
+            if ok(cores[j], cores[r]):
+                direct[j].append(r)
+            else:
+                m = min(m for m in own if m > j and ok(cores[j], cores[m]) and ok(cores[m], cores[r]))
+                fwd.setdefault((m, j), []).append(r)
+        for i in range(0, len(oth) - 1, 2):
+            want.setdefault((oth[i], oth[i + 1]), []).append(r)
+        if len(oth) % 2:
+            single[oth[-1]].append(r)
+
+    base = {cs(j): j for j in range(n)}
+    dpow = {}
+    raw_on = {j: [] for j in range(n)}
+    raw_off = {j: [] for j in range(n)}
+    d_on = {j: [] for j in range(n)}
+    d_off = {j: [] for j in range(n)}
+    hcalls = []
+    for (p, q), dsts in sorted(want.items()):
+        base[fs(p)] = q
+        dpow[p] = S * (q - p)
+        opts = {r: [m for m in (q, p) if any(ok(cores[p], k) and ok(cores[q], k) and ok(k, cores[r]) for k in chipc[m])]
+                for r in dsts}
+        agg = {}
+        for r in sorted(dsts, key=lambda r: (len(opts[r]), -r)):
+            m = min(opts[r], key=lambda m: (len(agg.get(m, [])), bool(single[m]) == bool(agg.get(m))))
+            agg.setdefault(m, []).append(r)
+        for m, rs in sorted(agg.items()):
+            early = single[m][:FAN]
+            h = pick(m, [cores[p], cores[q]], [cores[r] for r in rs + early])
+            (d_on if m == p else d_off)[p].append(h)
+            (raw_on if m == q else raw_off)[q].append(h)
+            if early:
+                single[m] = single[m][FAN:]
+                hcalls.append((h, 20, [cs(m)], cs(m), early, 0))
+                if m != q:
+                    raw_on[m].append(h)
+            elif m == q:
+                base[ds(p)] = q
+                hcalls.append((h, 20, [cs(q)], cs(q), rs[-1:], 0))
+                if rs[:-1]:
+                    hcalls.append((h, 30, [ds(p), cs(q)], fs(p), rs[:-1], 1))
+                hcalls.append((h, 31, [ds(p)], ds(p), rs[-1:], 0 if rs[:-1] else 1))
+                continue
+            hcalls.append((h, 30, [ds(p), cs(q)], fs(p), rs, 1 if early else None))
+    for j in range(n):
+        for i in range(0, len(single[j]), FAN):
+            rs = single[j][i:i + FAN]
+            h = pick(j, [cores[j]], [cores[r] for r in rs])
+            hcalls.append((h, 20, [cs(j)], cs(j), rs, None))
+            raw_on[j].append(h)
 
     calls, lands = {}, {}
 
     def add(core, needs, trs, score):
         calls.setdefault(core, []).append((needs, trs))
-        for s0, ns, dsts, mask in trs:
-            for p, d in enumerate(dsts):
-                lands.setdefault(d, []).append((score + p, s0, ns, bin(mask).count("1")))
+        for _, s, dsts, mask in trs:
+            for i, d in enumerate(dsts):
+                lands.setdefault(d, []).append((score + i, s, bin(mask).count("1")))
+
+    def both(c, s, off_d, on_d):
+        trs, off = [], 0
+        if off_d:
+            off = _engines(topo, c, off_d, NE_OFF, 0)
+            trs.append(([s], s, off_d, off))
+        if on_d:
+            trs.append(([s], s, on_d, _engines(topo, c, on_d, NE_ON, off)))
+        return trs
 
     for j in range(n - 1):
-        c, trs, off = cores[j], [], 0
-        if first[j][1]:
-            off = _engines(topo, c, first[j][1], NE_OFF, 0)
-            trs.append((slot[j], 1, first[j][1], off))
-        if first[j][0]:
-            trs.append((slot[j], 1, first[j][0], _engines(topo, c, first[j][0], NE_ON, off)))
+        c = cores[j]
+        passing = [r for r in direct[j] if (r, j) in fwd]
+        final = [cores[r] for r in direct[j] if r not in passing]
+        trs = both(c, cs(j), raw_off[j] + [cores[r] for r in passing], raw_on[j])
         if trs:
-            add(c, [], trs, 0)
-        if direct[j]:
-            dst = [cores[r] for r in direct[j]]
-            add(c, [], [(slot[j], 1, dst, _engines(topo, c, dst, NE_OFF, 0))], 5)
-        if j in fwd:
-            dst = [cores[r] for r in fwd[j][1]]
-            add(c, [fwd[j][0]], [(fwd[j][0], 1, dst, _engines(topo, c, dst, NE_OFF, 0))], 10)
-    for h, (score, needs, s0, ns, dst) in hcalls.items():
-        dst = [cores[r] for r in dst]
-        add(h, needs, [(s0, ns, dst, _engines(topo, h, dst, NE_OFF, 0))], score)
-    return slot, calls, lands
+            add(c, [cs(j)], trs, 0)
+        trs = both(c, ds(j), d_off[j], d_on[j])
+        if trs:
+            add(c, [ds(j)], trs, 0)
+        if final:
+            add(c, [cs(j)], [([cs(j)], cs(j), final, _engines(topo, c, final, NE_OFF, 0))], 5)
+        for (m, i), rs in sorted(fwd.items()):
+            if m == j:
+                dst = [cores[r] for r in rs]
+                add(c, [cs(i)], [([cs(i)], cs(i), dst, _engines(topo, c, dst, NE_OFF, 0))], 10)
+    for h, score, srcs, s, rs, part in hcalls:
+        dst = [cores[r] for r in rs]
+        if part is None:
+            mask = _engines(topo, h, dst, NE_OFF, 0)
+        else:
+            mask = _engines(topo, h, dst, NE_OFF // 2, 0)
+            if part:
+                mask = _engines(topo, h, dst, NE_OFF // 2, mask)
+        add(h, srcs, [(srcs, s, dst, mask)], score)
+    return calls, lands, base, dpow
 
 
-def _send(g, core, T, topo, calls, lands):
-    count = {s0: k for _, s0, _, k in lands}
+def _send(g, core, T, topo, calls, lands, own):
+    count = {s: k for _, s, k in lands}
     total = 0
     for needs, trs in calls:
         for s in needs:
-            g.wait_ge(T.sem["arr%d" % s], count[s])
+            if s in own:
+                g.wait_ge(own[s], 1)
+            else:
+                g.wait_ge(T.sem["arr%d" % s], count[s])
         lst = []
-        for s0, ns, dsts, mask in trs:
-            ap = T.land[:, s0 * B:(s0 + ns) * B]
+        for srcs, s, dsts, mask in trs:
             ids = []
             for d in dsts:
                 rid, pid = topo.addr(d, core)
                 ids.append(DstId(rid=rid, pnc=pid))
-            lst.append(RemoteDMATransfer(dst_ids=ids, dma_engine_mask=mask, remote_sem=T.sem["arr%d" % s0],
-                                         srcs=[ap], dsts=[ap for _ in dsts], alu_op=0))
+            lst.append(RemoteDMATransfer(dst_ids=ids, dma_engine_mask=mask, remote_sem=T.sem["arr%d" % s],
+                                         srcs=[T.land[:, i * B:(i + 1) * B] for i in srcs],
+                                         dsts=[T.land[:, s * B:(s + 1) * B] for _ in dsts],
+                                         alu_op=1 if len(srcs) > 1 else 0))
             total += bin(mask).count("1")
         g.remote_dma_fused(lst, local_sem=T.sem.loc)
     if total:
@@ -159,16 +208,18 @@ def _send(g, core, T, topo, calls, lands):
 def rank_program(g, core, T, topo):
     if "p" not in _CACHE:
         _CACHE["p"] = _plan(list(T.cores), topo)
-    slot, calls, lands = _CACHE["p"]
+    calls, lands, base, dpow = _CACHE["p"]
     rank = T.rank_of(core)
     if rank is None:
         if core in calls:
-            _send(g, core, T, topo, calls[core], lands[core])
+            _send(g, core, T, topo, calls[core], lands[core], {})
         return
 
     sem, te, ve, sy, sc = T.sem, g.tensor, g.vector, g.sync, g.scalar
     x0, x1 = T.xs[:, 0:B], T.xs[:, B:2 * B]
-    top = S * rank
+    seq = sorted(lands.get(core, []))
+    dh = dpow.get(rank, 0) // 2
+    top = max([S * (rank - base[s]) for _, s, _ in seq] + [dh])
 
     def pw(lo, hi):
         return T.pw[:, (lo - 1) * B:hi * B]
@@ -178,19 +229,56 @@ def rank_program(g, core, T, topo):
 
     sy.dma_start(T.xs[:], T.x[:]).then_inc(sem.ldx, 16)
     sc.dma_start(pw(1, 1), T.a[:]).then_inc(sem.lda, 16)
-    if top:
+    if top > 1:
         sc.dma_start(tp(0), T.at[:]).then_inc(sem.ldt, 16)
 
     te.wait_ge(sem.ldx, 16)
     te.wait_ge(sem.lda, 16)
     ve.wait_ge(sem.ldx, 16)
     if rank < N - 1:
-        mine = T.land[:, slot[rank] * B:(slot[rank] + 1) * B]
+        mine = T.land[:, rank * B:(rank + 1) * B]
+        dsl = T.land[:, (N - 1 + rank) * B:(N + rank) * B]
         te.matmul(T.pc[:, 0:B], pw(1, 1), x0, True, True).then_inc(sem.mmc, 1)
         ve.wait_ge(sem.mmc, 1)
         ve.tensor_tensor(mine, T.pc[:, 0:B], x1, AluOpType.add).then_inc(sem.car, 1)
-        g.wait_ge(sem.car, 1)
-        _send(g, core, T, topo, calls[core], lands.get(core, []))
+        _send(g, core, T, topo, calls[core], lands.get(core, []), {rank: sem.car, N - 1 + rank: sem.dd})
+
+    if top > 1:
+        te.wait_ge(sem.ldt, 16)
+    have, l, later = 1, 0, []
+    while have < top:
+        hi = min(2 * have, top)
+        mid = min(hi, have + 4)
+        pa, pt = T["pa%d" % (l % 2)], T["pt%d" % (l % 2)]
+        work = [(pw(have + 1, mid), pa[:, 0:(mid - have) * B], tp(l), pw(1, mid - have), "ma%d" % l, "ca%d" % l)]
+        if hi > mid:
+            work.append((pw(mid + 1, hi), pt[:, 0:(hi - mid) * B], tp(l), pw(mid - have + 1, hi - have),
+                         "mt%d" % l, "ct%d" % l))
+        elif hi < top:
+            work.insert(0 if have >= 4 else 1, (tp(l + 1), pt[:, 0:B], pw(have, have), tp(l), "mt%d" % l, "ct%d" % l))
+        for out, ps, lhs, rhs, sm, sv in work:
+            te.matmul(ps, lhs, rhs, True, True).then_inc(sem[sm], 1)
+            ve.wait_ge(sem[sm], 1)
+            ve.tensor_copy(out, ps).then_inc(sem[sv], 1)
+        nxt = min(2 * hi, top)
+        if max(nxt - hi, hi if nxt < top else 0) > have or have < dh <= mid:
+            te.wait_ge(sem["ca%d" % l], 1)
+        else:
+            later.append("ca%d" % l)
+        if have < dh <= mid:
+            te.wait_ge(sem.car, 1)
+            te.matmul(T.pc[:, 0:B], pw(dh, dh), mine, True, True).then_inc(sem.mq, 1)
+            ve.wait_ge(sem.mq, 1)
+            ve.tensor_copy(T.es[:], T.pc[:, 0:B]).then_inc(sem.cq, 1)
+            te.wait_ge(sem.cq, 1)
+            te.matmul(T.pd[:, 0:B], pw(dh, dh), T.es[:], True, True).then_inc(sem.md, 1)
+            ve.wait_ge(sem.md, 1)
+            ve.tensor_copy(dsl, T.pd[:, 0:B]).then_inc(sem.dd, 1)
+        if len(work) > 1:
+            te.wait_ge(sem["ct%d" % l], 1)
+        have, l = hi, l + 1
+    for s in later:
+        te.wait_ge(sem[s], 1)
 
     if rank == 0:
         sy.wait_ge(sem.ldx, 16)
@@ -204,40 +292,13 @@ def rank_program(g, core, T, topo):
     done = [0, 1]
     te.matmul(T.py1[:, 0:B], pw(1, 1), x0, True, False).then_inc(sem.my1, 1)
 
-    te.wait_ge(sem.ldt, 16)
-    have, l = 1, 0
-    while have < top:
-        hi = min(2 * have, top)
-        mid = min(hi, have + 4)
-        pa, pt = T["pa%d" % (l % 2)], T["pt%d" % (l % 2)]
-        te.matmul(pa[:, 0:(mid - have) * B], tp(l), pw(1, mid - have), True, True).then_inc(sem["ma%d" % l], 1)
-        ve.wait_ge(sem["ma%d" % l], 1)
-        ve.tensor_copy(pw(have + 1, mid), pa[:, 0:(mid - have) * B]).then_inc(sem["ca%d" % l], 1)
-        second = None
-        if hi > mid:
-            second = (pw(mid + 1, hi), pt[:, 0:(hi - mid) * B])
-            te.matmul(second[1], tp(l), pw(mid - have + 1, hi - have), True, True).then_inc(sem["mt%d" % l], 1)
-        elif hi < top:
-            second = (tp(l + 1), pt[:, 0:B])
-            te.matmul(second[1], pw(have, have), tp(l), True, True).then_inc(sem["mt%d" % l], 1)
-        if second:
-            ve.wait_ge(sem["mt%d" % l], 1)
-            ve.tensor_copy(second[0], second[1]).then_inc(sem["ct%d" % l], 1)
-            te.wait_ge(sem["ct%d" % l], 1)
-        te.wait_ge(sem["ca%d" % l], 1)
-        have, l = hi, l + 1
-
-    piece = {s: j for j, s in slot.items()}
-    seq = sorted(lands[core])
-    for i, (_, s0, ns, cnt) in enumerate(seq):
-        te.wait_ge(sem["arr%d" % s0], cnt)
+    for i, (_, s, cnt) in enumerate(seq):
+        te.wait_ge(sem["arr%d" % s], cnt)
         for half in range(S):
-            for s in range(s0, s0 + ns):
-                k = S * (rank - 1 - piece[s]) + 1 + half
-                last = i == len(seq) - 1 and s == s0 + ns - 1
-                te.matmul(T["py%d" % half][:, 0:B], pw(k, k), T.land[:, s * B:(s + 1) * B],
-                          done[half] == 0, last).then_inc(sem["my%d" % half], 1)
-                done[half] += 1
+            k = S * (rank - 1 - base[s]) + 1 + half
+            te.matmul(T["py%d" % half][:, 0:B], pw(k, k), T.land[:, s * B:(s + 1) * B],
+                      done[half] == 0, i == len(seq) - 1).then_inc(sem["my%d" % half], 1)
+            done[half] += 1
 
     ve.wait_ge(sem.my0, done[0])
     ve.tensor_tensor(T.ys[:, 0:B], T.py0[:, 0:B], x0, AluOpType.add).then_inc(sem.vy0, 1)

from concourse.bass import DstId, RemoteDMATransfer
from concourse.mybir import AluOpType

N, S, B = 8, 2, 128
WORLD = 512
NPOW = S * (N - 1)
FAN = 2
NE_OFF = 8
NE_ON = 8
LEVELS = 4
NSLOT = 3 * (N - 1)

SCRATCH = {
    "xs": ("sbuf", [128, S * B], "bfloat16"),
    "pw": ("sbuf", [128, NPOW * B], "bfloat16"),
    "tp": ("sbuf", [128, LEVELS * B], "bfloat16"),
    "land": ("sbuf", [128, NSLOT * B], "bfloat16"),
    "es": ("sbuf", [128, B], "bfloat16"),
    "ys": ("sbuf", [128, S * B], "bfloat16"),
    "pc": ("psum", [128, 512], "float32"),
    "pd": ("psum", [128, 512], "float32"),
    "py0": ("psum", [128, 512], "float32"),
    "py1": ("psum", [128, 512], "float32"),
    "pa0": ("psum", [128, 512], "float32"),
    "pa1": ("psum", [128, 512], "float32"),
    "pt0": ("psum", [128, 512], "float32"),
    "pt1": ("psum", [128, 512], "float32"),
}
SEMAPHORES = (["ldx", "lda", "ldt", "mmc", "car", "mq", "cq", "md", "dd", "my0", "my1", "vy0", "vy1", "st0", "st1", "loc"]
              + ["arr%d" % s for s in range(NSLOT)]
              + ["%s%d" % (n, l) for l in range(LEVELS) for n in ("ma", "mt", "ca", "ct")])

_CACHE = {}


def _same_chip(topo, a, b):
    return topo.host(a) == topo.host(b) and topo.chip(a) == topo.chip(b)


def _engines(topo, src, dsts, count, avoid):
    m = topo.mask(src, dsts[0])
    for d in dsts[1:]:
        m &= topo.mask(src, d)
    free = [i for i in range(m.bit_length()) if (m >> i) & 1 and not (avoid >> i) & 1]
    out = 0
    for i in free[:count]:
        out |= 1 << i
    return out


def _plan(cores, topo):
    n = len(cores)
    ok = topo.may_write
    chipc = [[k for k in range(WORLD) if k != c and _same_chip(topo, k, c)] for c in cores]
    used = []

    def cs(j):
        return j

    def ds(j):
        return n - 1 + j

    def fs(j):
        return 2 * (n - 1) + j

    def pick(m, srcs, dsts):
        cand = [k for k in chipc[m] if k not in used and all(ok(s, k) for s in srcs) and all(ok(k, d) for d in dsts)]
        cand.sort(key=lambda k: (topo.die(k) != topo.die(cores[m]), k))
        used.append(cand[0])
        return cand[0]

    cls = list(range(n))
    for i in range(n):
        for j in range(i):
            if ok(cores[j], cores[i]) and cls[i] != cls[j]:
                old, new = cls[i], cls[j]
                cls = [new if c == old else c for c in cls]

    direct = {j: [] for j in range(n)}
    fwd = {}
    want = {}
    single = {j: [] for j in range(n)}
    for r in range(n):
        own = [j for j in range(r) if cls[j] == cls[r]]
        oth = [j for j in range(r) if cls[j] != cls[r]]
        for j in own:
            if ok(cores[j], cores[r]):
                direct[j].append(r)
            else:
                m = min(m for m in own if m > j and ok(cores[j], cores[m]) and ok(cores[m], cores[r]))
                fwd.setdefault((m, j), []).append(r)
        for i in range(0, len(oth) - 1, 2):
            want.setdefault((oth[i], oth[i + 1]), []).append(r)
        if len(oth) % 2:
            single[oth[-1]].append(r)

    base = {cs(j): j for j in range(n)}
    dpow = {}
    raw_on = {j: [] for j in range(n)}
    raw_off = {j: [] for j in range(n)}
    d_on = {j: [] for j in range(n)}
    d_off = {j: [] for j in range(n)}
    hcalls = []
    for (p, q), dsts in sorted(want.items()):
        base[fs(p)] = q
        dpow[p] = S * (q - p)
        opts = {r: [m for m in (q, p) if any(ok(cores[p], k) and ok(cores[q], k) and ok(k, cores[r]) for k in chipc[m])]
                for r in dsts}
        agg = {}
        for r in sorted(dsts, key=lambda r: (len(opts[r]), -r)):
            m = min(opts[r], key=lambda m: (len(agg.get(m, [])), bool(single[m]) == bool(agg.get(m))))
            agg.setdefault(m, []).append(r)
        for m, rs in sorted(agg.items()):
            early = single[m][:FAN]
            h = pick(m, [cores[p], cores[q]], [cores[r] for r in rs + early])
            (d_on if m == p else d_off)[p].append(h)
            (raw_on if m == q else raw_off)[q].append(h)
            if early:
                single[m] = single[m][FAN:]
                hcalls.append((h, 20, [cs(m)], cs(m), early, 0))
                if m != q:
                    raw_on[m].append(h)
            elif m == q:
                base[ds(p)] = q
                hcalls.append((h, 20, [cs(q)], cs(q), rs[-1:], 0))
                if rs[:-1]:
                    hcalls.append((h, 30, [ds(p), cs(q)], fs(p), rs[:-1], 1))
                hcalls.append((h, 31, [ds(p)], ds(p), rs[-1:], 0 if rs[:-1] else 1))
                continue
            hcalls.append((h, 30, [ds(p), cs(q)], fs(p), rs, 1 if early else None))
    for j in range(n):
        for i in range(0, len(single[j]), FAN):
            rs = single[j][i:i + FAN]
            h = pick(j, [cores[j]], [cores[r] for r in rs])
            hcalls.append((h, 20, [cs(j)], cs(j), rs, None))
            raw_on[j].append(h)

    calls, lands = {}, {}

    def add(core, needs, trs, score):
        calls.setdefault(core, []).append((needs, trs))
        for _, s, dsts, mask in trs:
            for i, d in enumerate(dsts):
                lands.setdefault(d, []).append((score + i, s, bin(mask).count("1")))

    def both(c, s, off_d, on_d):
        trs, off = [], 0
        if off_d:
            off = _engines(topo, c, off_d, NE_OFF, 0)
            trs.append(([s], s, off_d, off))
        if on_d:
            trs.append(([s], s, on_d, _engines(topo, c, on_d, NE_ON, off)))
        return trs

    for j in range(n - 1):
        c = cores[j]
        passing = [r for r in direct[j] if (r, j) in fwd]
        final = [cores[r] for r in direct[j] if r not in passing]
        trs = both(c, cs(j), raw_off[j] + [cores[r] for r in passing], raw_on[j])
        if trs:
            add(c, [cs(j)], trs, 0)
        trs = both(c, ds(j), d_off[j], d_on[j])
        if trs:
            add(c, [ds(j)], trs, 0)
        if final:
            add(c, [cs(j)], [([cs(j)], cs(j), final, _engines(topo, c, final, NE_OFF, 0))], 5)
        for (m, i), rs in sorted(fwd.items()):
            if m == j:
                dst = [cores[r] for r in rs]
                add(c, [cs(i)], [([cs(i)], cs(i), dst, _engines(topo, c, dst, NE_OFF, 0))], 10)
    for h, score, srcs, s, rs, part in hcalls:
        dst = [cores[r] for r in rs]
        if part is None:
            mask = _engines(topo, h, dst, NE_OFF, 0)
        else:
            mask = _engines(topo, h, dst, NE_OFF // 2, 0)
            if part:
                mask = _engines(topo, h, dst, NE_OFF // 2, mask)
        add(h, srcs, [(srcs, s, dst, mask)], score)
    return calls, lands, base, dpow


def _send(g, core, T, topo, calls, lands, own):
    count = {s: k for _, s, k in lands}
    total = 0
    for needs, trs in calls:
        for s in needs:
            if s in own:
                g.wait_ge(own[s], 1)
            else:
                g.wait_ge(T.sem["arr%d" % s], count[s])
        lst = []
        for srcs, s, dsts, mask in trs:
            ids = []
            for d in dsts:
                rid, pid = topo.addr(d, core)
                ids.append(DstId(rid=rid, pnc=pid))
            lst.append(RemoteDMATransfer(dst_ids=ids, dma_engine_mask=mask, remote_sem=T.sem["arr%d" % s],
                                         srcs=[T.land[:, i * B:(i + 1) * B] for i in srcs],
                                         dsts=[T.land[:, s * B:(s + 1) * B] for _ in dsts],
                                         alu_op=1 if len(srcs) > 1 else 0))
            total += bin(mask).count("1")
        g.remote_dma_fused(lst, local_sem=T.sem.loc)
    if total:
        g.wait_ge(T.sem.loc, total)


def rank_program(g, core, T, topo):
    if "p" not in _CACHE:
        _CACHE["p"] = _plan(list(T.cores), topo)
    calls, lands, base, dpow = _CACHE["p"]
    rank = T.rank_of(core)
    if rank is None:
        if core in calls:
            _send(g, core, T, topo, calls[core], lands[core], {})
        return

    sem, te, ve, sy, sc = T.sem, g.tensor, g.vector, g.sync, g.scalar
    x0, x1 = T.xs[:, 0:B], T.xs[:, B:2 * B]
    seq = sorted(lands.get(core, []))
    dh = dpow.get(rank, 0) // 2
    top = max([S * (rank - base[s]) for _, s, _ in seq] + [dh])

    def pw(lo, hi):
        return T.pw[:, (lo - 1) * B:hi * B]

    def tp(i):
        return T.tp[:, i * B:(i + 1) * B]

    sy.dma_start(T.xs[:], T.x[:]).then_inc(sem.ldx, 16)
    sc.dma_start(pw(1, 1), T.a[:]).then_inc(sem.lda, 16)
    if top > 1:
        sc.dma_start(tp(0), T.at[:]).then_inc(sem.ldt, 16)

    te.wait_ge(sem.ldx, 16)
    te.wait_ge(sem.lda, 16)
    ve.wait_ge(sem.ldx, 16)
    if rank < N - 1:
        mine = T.land[:, rank * B:(rank + 1) * B]
        dsl = T.land[:, (N - 1 + rank) * B:(N + rank) * B]
        te.matmul(T.pc[:, 0:B], pw(1, 1), x0, True, True).then_inc(sem.mmc, 1)
        ve.wait_ge(sem.mmc, 1)
        ve.tensor_tensor(mine, T.pc[:, 0:B], x1, AluOpType.add).then_inc(sem.car, 1)
        _send(g, core, T, topo, calls[core], lands.get(core, []), {rank: sem.car, N - 1 + rank: sem.dd})

    if top > 1:
        te.wait_ge(sem.ldt, 16)
    have, l, later = 1, 0, []
    while have < top:
        hi = min(2 * have, top)
        mid = min(hi, have + 4)
        pa, pt = T["pa%d" % (l % 2)], T["pt%d" % (l % 2)]
        work = [(pw(have + 1, mid), pa[:, 0:(mid - have) * B], tp(l), pw(1, mid - have), "ma%d" % l, "ca%d" % l)]
        if hi > mid:
            work.append((pw(mid + 1, hi), pt[:, 0:(hi - mid) * B], tp(l), pw(mid - have + 1, hi - have),
                         "mt%d" % l, "ct%d" % l))
        elif hi < top:
            work.insert(0 if have >= 4 else 1, (tp(l + 1), pt[:, 0:B], pw(have, have), tp(l), "mt%d" % l, "ct%d" % l))
        for out, ps, lhs, rhs, sm, sv in work:
            te.matmul(ps, lhs, rhs, True, True).then_inc(sem[sm], 1)
            ve.wait_ge(sem[sm], 1)
            ve.tensor_copy(out, ps).then_inc(sem[sv], 1)
        nxt = min(2 * hi, top)
        if max(nxt - hi, hi if nxt < top else 0) > have or have < dh <= mid:
            te.wait_ge(sem["ca%d" % l], 1)
        else:
            later.append("ca%d" % l)
        if have < dh <= mid:
            te.wait_ge(sem.car, 1)
            te.matmul(T.pc[:, 0:B], pw(dh, dh), mine, True, True).then_inc(sem.mq, 1)
            ve.wait_ge(sem.mq, 1)
            ve.tensor_copy(T.es[:], T.pc[:, 0:B]).then_inc(sem.cq, 1)
            te.wait_ge(sem.cq, 1)
            te.matmul(T.pd[:, 0:B], pw(dh, dh), T.es[:], True, True).then_inc(sem.md, 1)
            ve.wait_ge(sem.md, 1)
            ve.tensor_copy(dsl, T.pd[:, 0:B]).then_inc(sem.dd, 1)
        if len(work) > 1:
            te.wait_ge(sem["ct%d" % l], 1)
        have, l = hi, l + 1
    for s in later:
        te.wait_ge(sem[s], 1)

    if rank == 0:
        sy.wait_ge(sem.ldx, 16)
        sy.dma_start(T.y[:, 0:B], x0).then_inc(sem.st0, 16)
        sy.wait_ge(sem.st0, 16)
        sc.wait_ge(sem.car, 1)
        sc.dma_start(T.y[:, B:2 * B], mine).then_inc(sem.st1, 16)
        sc.wait_ge(sem.st1, 16)
        return

    done = [0, 1]
    te.matmul(T.py1[:, 0:B], pw(1, 1), x0, True, False).then_inc(sem.my1, 1)

    for i, (_, s, cnt) in enumerate(seq):
        te.wait_ge(sem["arr%d" % s], cnt)
        for half in range(S):
            k = S * (rank - 1 - base[s]) + 1 + half
            te.matmul(T["py%d" % half][:, 0:B], pw(k, k), T.land[:, s * B:(s + 1) * B],
                      done[half] == 0, i == len(seq) - 1).then_inc(sem["my%d" % half], 1)
            done[half] += 1

    ve.wait_ge(sem.my0, done[0])
    ve.tensor_tensor(T.ys[:, 0:B], T.py0[:, 0:B], x0, AluOpType.add).then_inc(sem.vy0, 1)
    ve.wait_ge(sem.my1, done[1])
    ve.tensor_tensor(T.ys[:, B:2 * B], T.py1[:, 0:B], x1, AluOpType.add).then_inc(sem.vy1, 1)
    sy.wait_ge(sem.vy0, 1)
    sy.dma_start(T.y[:, 0:B], T.ys[:, 0:B]).then_inc(sem.st0, 16)
    sy.wait_ge(sem.st0, 16)
    sc.wait_ge(sem.vy1, 1)
    sc.dma_start(T.y[:, B:2 * B], T.ys[:, B:2 * B]).then_inc(sem.st1, 16)
    sc.wait_ge(sem.st1, 16)
